import numpy as np
import ml_dtypes


def mxq(x, axis, fmt="e4m3"):
    dtype, down = {"e4m3": (ml_dtypes.float8_e4m3fn, 7), "e5m2": (ml_dtypes.float8_e5m2, 14)}[fmt]
    v = np.moveaxis(np.asarray(x, np.float32).astype(ml_dtypes.bfloat16).astype(np.float64), axis, -1)
    blocks = v.reshape(v.shape[:-1] + (-1, 32))
    amax = np.abs(blocks).max(-1, keepdims=True)
    byte = np.maximum(np.where(amax > 0, np.frexp(amax)[1] - 1 + 127, 0) - down, 1)
    scale = np.exp2(byte - 127.0)
    codes = (blocks / scale).astype(np.float32).astype(dtype).astype(np.float64)
    return np.moveaxis((codes * scale).reshape(v.shape), -1, axis)


WIDE = False


def mx_kscale(k):
    if not WIDE:
        return np.ones(k)
    levels = np.array([30, -30])
    if k % 512:
        return np.exp2(np.random.permutation(np.resize(levels, k // 32))).repeat(32)
    a = np.empty((k // 512, 16))
    for p in range(k // 512):
        a[p, :8] = np.random.permutation(np.resize(levels, 8))
        for g in range(8):
            far = levels[np.abs(levels - a[p, g]) >= 10]
            a[p, g + 8] = far[np.random.randint(len(far))]
    return np.exp2(a.ravel()).repeat(32)


def f64(x):
    return np.asarray(x).astype(np.float64)


def striped(idx):
    return np.tile(np.asarray(idx).reshape(-1, 16).T, (8, 1)).astype(np.uint16)


def unstriped(offs):
    return offs[:16].T.reshape(-1).astype(np.int64)


E2M1 = np.array([0.0, 0.5, 1.0, 1.5, 2.0, 3.0, 4.0, 6.0, -0.0, -0.5, -1.0, -1.5, -2.0, -3.0, -4.0, -6.0])


def pack_weight(w, fmt):
    k, n = w.shape
    w = f64(np.asarray(w, np.float32).astype(ml_dtypes.bfloat16)).reshape(k // 32, 32, n)
    amax = np.abs(w).max(1)
    if fmt in ("e4m3", "e5m2"):
        byte = np.frexp(amax)[1] - 1 + 127 - (7 if fmt == "e4m3" else 14)
    else:
        mant, ex = np.frexp(amax / 6.0)
        byte = np.where(mant > 0.5, ex, ex - 1) + 127
    byte = np.clip(np.where(amax > 0, byte, 1), 1, 254)
    scaled = (w * np.exp2(127.0 - byte)[:, None, :]).reshape(k, n).astype(np.float32)
    by_word = np.ascontiguousarray(scaled.reshape(k // 512, 128, 4, n).transpose(0, 1, 3, 2))
    if fmt in ("e4m3", "e5m2"):
        words = by_word.astype(ml_dtypes.float8_e4m3fn if fmt == "e4m3" else ml_dtypes.float8_e5m2).view(np.uint8)
    else:
        c = by_word.astype(ml_dtypes.float4_e2m1fn).view(np.uint8) & 0xF
        words = (c[..., 0::2] | (c[..., 1::2] << 4)).reshape(k // 512, 128, 2 * n)
    return np.ascontiguousarray(words), np.ascontiguousarray(byte.astype(np.uint8).reshape(k // 512, 16, n))


def unpack_weight(words, scales, fmt):
    g, _, n = scales.shape
    words = np.ascontiguousarray(words).reshape(g, 128, n, -1)
    if fmt in ("e4m3", "e5m2"):
        vals = words.view(ml_dtypes.float8_e4m3fn if fmt == "e4m3" else ml_dtypes.float8_e5m2).astype(np.float64)
    else:
        nib = np.empty((g, 128, n, 4), np.uint8)
        nib[..., 0::2] = words & 0xF
        nib[..., 1::2] = words >> 4
        vals = E2M1[nib]
    vals = vals * np.repeat(np.exp2(scales.astype(np.float64) - 127.0), 8, axis=1)[..., None]
    return vals.transpose(0, 1, 3, 2).reshape(g * 512, n)


def sgn(shape):
    return np.random.uniform(0.5, 2.0, shape) * np.where(np.random.standard_normal(shape) < 0, -1.0, 1.0)


K, T, J, R, V, O, N, E = 512, 1024, 256, 512, 1024, 128, 256, 256


def setup_inputs():
    n = np.random.standard_normal
    idx = np.random.permutation(V)[:R]
    idx2 = np.random.permutation(T)[:J]
    idx3 = np.random.permutation(J)[:O]
    idx4 = np.random.permutation(E)[:O]
    idx5 = np.random.permutation(E)[:O]
    fk = mx_kscale(K)
    fr = mx_kscale(R)
    xtp = pack_weight(n((K, T)) / fk[:, None], "e2m1")
    wtp = pack_weight(n((K, V)) * 1 / np.sqrt(K) * fk[:, None], "e5m2")
    wbp = pack_weight(n((R, N)) * 1 / np.sqrt(R) / fr[:, None], "e4m3")
    wcp = pack_weight(n((R, N)) * 1 / np.sqrt(R) / fr[:, None], "e2m1")
    return {
        "xt_words": xtp[0],
        "xt_scales": xtp[1],
        "wt_words": wtp[0],
        "wt_scales": wtp[1],
        "sa": (sgn((R, 1)) * fr[:, None]).astype(np.float32),
        "wb_words": wbp[0],
        "wb_scales": wbp[1],
        "wc_words": wcp[0],
        "wc_scales": wcp[1],
        "so": (np.random.uniform(0.5, 1.6, (N, 1))).astype(np.float32),
        "sp": (np.random.uniform(0.5, 1.6, (N, 1))).astype(np.float32),
        "offs": striped(idx),
        "offs2": striped(idx2),
        "offs3": striped(idx3),
        "offs4": striped(idx4),
        "offs5": striped(idx5),
    }


def reference(xt_words, xt_scales, wt_words, wt_scales, sa, wb_words, wb_scales, wc_words, wc_scales, so, sp, offs, offs2, offs3, offs4, offs5):
    idx = unstriped(offs)
    idx2 = unstriped(offs2)
    idx3 = unstriped(offs3)
    idx4 = unstriped(offs4)
    idx5 = unstriped(offs5)
    xtu = unpack_weight(xt_words, xt_scales, "e2m1")
    wtu = unpack_weight(wt_words, wt_scales, "e5m2")
    wbu = unpack_weight(wb_words, wb_scales, "e4m3")
    wcu = unpack_weight(wc_words, wc_scales, "e2m1")
    wtidxg = wtu[:, idx]
    xtidx2g = xtu[:, idx2]
    a = wtidxg.T @ xtidx2g
    hid = a[:, idx3] * f64(sa)
    hidq = mxq(hid, 0, "e5m2")
    p = wbu.T @ hidq
    q = wcu.T @ hidq
    pa = np.zeros((N, E))
    pa[:, idx4] = p * f64(so)
    pb = np.zeros((N, E))
    pb[:, idx5] = q * f64(sp)
    y = np.maximum(pa, pb)
    return y

@@ -1,0 +1,134 @@
+from contextlib import ExitStack
+
+import concourse.mybir as mybir
+
+K, T, J, R, V, O, N, E = 512, 1024, 256, 512, 1024, 128, 256, 256
+FLOPS = 2 * K * R * J + 2 * 2 * R * N * O
+
+P = 128
+PACK = 4
+QUADS = 4
+QUAD = 32
+
+F32 = mybir.dt.float32
+BF16 = mybir.dt.bfloat16
+I32 = mybir.dt.int32
+U32 = mybir.dt.uint32
+U16 = mybir.dt.uint16
+U8 = mybir.dt.uint8
+E4M3 = mybir.dt.float8_e4m3fn_x4
+E5M2 = mybir.dt.float8_e5m2_x4
+E2M1 = mybir.dt.float4_e2m1fn_x4
+COPY = mybir.ActivationFunctionType.Copy
+MAX = mybir.AluOpType.max
+
+
+def tile_list_twooutcomes_kernel(tc, xt_words, xt_scales, wt_words, wt_scales, sa, wb_words, wb_scales,
+                                     wc_words, wc_scales, so, sp, offs, offs2, offs3, offs4, offs5, out):
+    nc = tc.nc
+    with ExitStack() as ctx:
+        sb = ctx.enter_context(tc.tile_pool(name="sb", bufs=1))
+        ps = ctx.enter_context(tc.psum_pool(name="ps", bufs=1))
+
+        def tile(name, cols, dtype):
+            return sb.tile([P, cols], dtype, name=name, align_bytes=64)
+
+        def load_scale_rows(queues, plane, scales):
+            for q, queue in enumerate(queues):
+                queue.dma_start(out=plane[QUAD * q : QUAD * q + 4, :].bitcast(I32),
+                                in_=scales[0, 4 * q : 4 * q + 4, :].bitcast(I32))
+
+        r_list = tile("r_list", R // 16, U16)
+        j_list = tile("j_list", J // 16, U16)
+        o_list = tile("o_list", O // 16, U16)
+        pa_list = tile("pa_list", O // 16, U16)
+        pb_list = tile("pb_list", O // 16, U16)
+        wt_w = tile("wt_w", V, U32)
+        wt_s = tile("wt_s", V, U8)
+        xt_w = tile("xt_w", T, U16)
+        xt_s = tile("xt_s", T, U8)
+        wb_w = tile("wb_w", N, U32)
+        wb_s = tile("wb_s", N, U8)
+        wc_w = tile("wc_w", 2 * N, U8)
+        wc_s = tile("wc_s", N, U8)
+        sa_t = tile("sa_t", PACK, F32)
+        so_t = tile("so_t", 2, F32)
+        sp_t = tile("sp_t", 2, F32)
+        pages = [[tile("page_%d_%d" % (s, h), E, F32) for h in range(2)] for s in range(2)]
+
+        nc.vector.memset(wt_s[:].bitcast(I32), 0)
+        nc.vector.memset(xt_s[:].bitcast(I32), 0)
+        nc.vector.memset(wb_s[:].bitcast(I32), 0)
+        nc.vector.memset(wc_s[:].bitcast(I32), 0)
+        for h in range(2):
+            for s in range(2):
+                nc.vector.memset(pages[s][h][:], 0.0)
+
+        nc.sync.dma_start(j_list[:], offs2)
+        nc.sync.dma_start(out=xt_w[:].bitcast(I32), in_=xt_words[0].bitcast(I32))
+        nc.sync.dma_start(r_list[:], offs)
+        load_scale_rows([nc.scalar, nc.sync, nc.scalar, nc.sync], wt_s, wt_scales)
+        nc.sync.dma_start(out=wt_w[:].bitcast(I32), in_=wt_words[0].rearrange("p n t -> p (n t)").bitcast(I32))
+        load_scale_rows([nc.sync] * QUADS, xt_s, xt_scales)
+        nc.sync.dma_start(o_list[:], offs3)
+        nc.sync.dma_start(out=sa_t[:], in_=sa.rearrange("(p t) o -> p (t o)", t=PACK))
+        nc.sync.dma_start(out=wb_w[:].bitcast(I32), in_=wb_words[0].rearrange("p n t -> p (n t)").bitcast(I32))
+        nc.sync.dma_start(out=wc_w[:].bitcast(I32), in_=wc_words[0].bitcast(I32))
+        load_scale_rows([nc.sync] * QUADS, wb_s, wb_scales)
+        load_scale_rows([nc.sync] * QUADS, wc_s, wc_scales)
+        nc.sync.dma_start(pa_list[:], offs4)
+        with nc.allow_non_contiguous_dma(reason="one value a partition and half"):
+            nc.sync.dma_start(out=so_t[:], in_=so.rearrange("(h p) o -> p (h o)", h=2))
+            nc.sync.dma_start(pb_list[:], offs5)
+            nc.sync.dma_start(out=sp_t[:], in_=sp.rearrange("(h p) o -> p (h o)", h=2))
+
+        wg_w = tile("wg_w", R, U32)
+        wg_s = tile("wg_s", R, U8)
+        xg_w = tile("xg_w", J, U16)
+        xg_s = tile("xg_s", J, U8)
+        nc.vector.tensor_copy(xg_w[:], xt_w[:].indirect(j_list[:]))
+        nc.vector.tensor_copy(wg_s[:].rearrange("p (t q) -> p q t", t=PACK), wt_s[:].indirect(r_list[:]))
+        nc.vector.tensor_copy(wg_w[:].rearrange("p (t q) -> p q t", t=PACK), wt_w[:].indirect(r_list[:]))
+        nc.vector.tensor_copy(xg_s[:], xt_s[:].indirect(j_list[:]))
+
+        hid = tile("hid", PACK * O, BF16)
+        for t in range(PACK):
+            cols = slice(P * t, P * (t + 1))
+            a_sb = tile("a_sb_%d" % t, J, F32)
+            parts = 2 if t == 0 else 1
+            for c in range(parts):
+                js = slice(J // parts * c, J // parts * (c + 1))
+                a_ps = ps.tile([P, J // parts], F32, name="a_ps_%d_%d" % (t, c), tag="bank_%d" % (t + 4 * c))
+                nc.tensor.matmul_mx(out=a_ps[:], lhsT=wg_w[:, cols].bitcast(E5M2), lhsT_scale=wg_s[:, cols],
+                                    rhs=xg_w[:, js].bitcast(E2M1), rhs_scale=xg_s[:, js], start=True, stop=True)
+                if c == 0:
+                    nc.vector.tensor_copy(a_sb[:, js], a_ps[:])
+                else:
+                    nc.scalar.activation(out=a_sb[:, js], in_=a_ps[:], func=COPY)
+            nc.scalar.activation(out=hid[:, t : PACK * O : PACK], in_=a_sb[:].indirect(o_list[:]), func=COPY,
+                                 scale=sa_t[:, t : t + 1])
+
+        hid_w = tile("hid_w", O, U32)
+        hid_s = tile("hid_s", O, U8)
+        nc.vector.quantize_mx(out=hid_w[:].bitcast(E5M2), scales=hid_s[:], in_=hid[:])
+
+        for h in range(2):
+            cols = slice(P * h, P * (h + 1))
+            sides = (
+                (wb_w[:, cols].bitcast(E4M3), wb_s[:, cols], so_t, pa_list),
+                (wc_w[:, 2 * P * h : 2 * P * (h + 1)].bitcast(E2M1), wc_s[:, cols], sp_t, pb_list),
+            )
+            for s, (words, scales, weight, places) in enumerate(sides):
+                y_ps = ps.tile([P, O], F32, name="y_ps_%d_%d" % (s, h), tag="bank_%d" % (4 + 2 * h + s))
+                nc.tensor.matmul_mx(out=y_ps[:], lhsT=words, lhsT_scale=scales, rhs=hid_w[:].bitcast(E5M2),
+                                    rhs_scale=hid_s[:], start=True, stop=True)
+                y_sb = tile("y_sb_%d_%d" % (s, h), O, F32)
+                nc.vector.tensor_copy(y_sb[:], y_ps[:])
+                nc.scalar.activation(out=pages[s][h][:].indirect(places[:]), in_=y_sb[:], func=COPY,
+                                     scale=weight[:, h : h + 1])
+            queues = (nc.sync,) if h == 0 else (nc.sync, nc.scalar)
+            for c, queue in enumerate(queues):
+                half = slice(E // len(queues) * c, E // len(queues) * (c + 1))
+                best = tile("best_%d_%d" % (h, c), E // len(queues), F32)
+                nc.vector.tensor_tensor(best[:], pages[0][h][:, half], pages[1][h][:, half], MAX)
+                queue.dma_start(out=out[cols, half], in_=best[:])

@@ -64,8 +64,8 @@ def tile_list_twooutcomes_kernel(tc, xt_words, xt_scales, wt_words, wt_scales, s
             for s in range(2):
                 nc.vector.memset(pages[s][h][:], 0.0)
 
-        nc.sync.dma_start(j_list[:], offs2)
         nc.sync.dma_start(out=xt_w[:].bitcast(I32), in_=xt_words[0].bitcast(I32))
+        nc.sync.dma_start(j_list[:], offs2)
         nc.sync.dma_start(r_list[:], offs)
         load_scale_rows([nc.scalar, nc.sync, nc.scalar, nc.sync], wt_s, wt_scales)
         nc.sync.dma_start(out=wt_w[:].bitcast(I32), in_=wt_words[0].rearrange("p n t -> p (n t)").bitcast(I32))
@@ -75,11 +75,12 @@ def tile_list_twooutcomes_kernel(tc, xt_words, xt_scales, wt_words, wt_scales, s
         nc.sync.dma_start(out=wb_w[:].bitcast(I32), in_=wb_words[0].rearrange("p n t -> p (n t)").bitcast(I32))
         nc.sync.dma_start(out=wc_w[:].bitcast(I32), in_=wc_words[0].bitcast(I32))
         load_scale_rows([nc.sync] * QUADS, wb_s, wb_scales)
-        load_scale_rows([nc.sync] * QUADS, wc_s, wc_scales)
         nc.sync.dma_start(pa_list[:], offs4)
         with nc.allow_non_contiguous_dma(reason="one value a partition and half"):
             nc.sync.dma_start(out=so_t[:], in_=so.rearrange("(h p) o -> p (h o)", h=2))
-            nc.sync.dma_start(pb_list[:], offs5)
+        load_scale_rows([nc.sync] * QUADS, wc_s, wc_scales)
+        nc.sync.dma_start(pb_list[:], offs5)
+        with nc.allow_non_contiguous_dma(reason="one value a partition and half"):
             nc.sync.dma_start(out=sp_t[:], in_=sp.rearrange("(h p) o -> p (h o)", h=2))
 
         wg_w = tile("wg_w", R, U32)
@@ -89,46 +90,49 @@ def tile_list_twooutcomes_kernel(tc, xt_words, xt_scales, wt_words, wt_scales, s
         nc.vector.tensor_copy(xg_w[:], xt_w[:].indirect(j_list[:]))
         nc.vector.tensor_copy(wg_s[:].rearrange("p (t q) -> p q t", t=PACK), wt_s[:].indirect(r_list[:]))
         nc.vector.tensor_copy(wg_w[:].rearrange("p (t q) -> p q t", t=PACK), wt_w[:].indirect(r_list[:]))
-        nc.vector.tensor_copy(xg_s[:], xt_s[:].indirect(j_list[:]))
+        for c in range(2):
+            nc.vector.tensor_copy(xg_s[:, J // 2 * c : J // 2 * (c + 1)],
+                                  xt_s[:].indirect(j_list[:, J // 32 * c : J // 32 * (c + 1)]))
 
         hid = tile("hid", PACK * O, BF16)
-        for t in range(PACK):
+        a_sb = [tile("a_sb_%d" % t, J, F32) for t in range(PACK)]
+        halves = (slice(0, J // 2), slice(J // 2, J))
+        products = [(t, js) for js in halves for t in range(2)] + [(t, slice(0, J)) for t in range(2, PACK)]
+        for bank, (t, js) in enumerate(products):
             cols = slice(P * t, P * (t + 1))
-            a_sb = tile("a_sb_%d" % t, J, F32)
-            parts = 2 if t == 0 else 1
-            for c in range(parts):
-                js = slice(J // parts * c, J // parts * (c + 1))
-                a_ps = ps.tile([P, J // parts], F32, name="a_ps_%d_%d" % (t, c), tag="bank_%d" % (t + 4 * c))
-                nc.tensor.matmul_mx(out=a_ps[:], lhsT=wg_w[:, cols].bitcast(E5M2), lhsT_scale=wg_s[:, cols],
-                                    rhs=xg_w[:, js].bitcast(E2M1), rhs_scale=xg_s[:, js], start=True, stop=True)
-                if c == 0:
-                    nc.vector.tensor_copy(a_sb[:, js], a_ps[:])
-                else:
-                    nc.scalar.activation(out=a_sb[:, js], in_=a_ps[:], func=COPY)
-            nc.scalar.activation(out=hid[:, t : PACK * O : PACK], in_=a_sb[:].indirect(o_list[:]), func=COPY,
+            a_ps = ps.tile([P, js.stop - js.start], F32, name="a_ps_%d" % bank, tag="bank_%d" % bank)
+            nc.tensor.matmul_mx(out=a_ps[:], lhsT=wg_w[:, cols].bitcast(E5M2), lhsT_scale=wg_s[:, cols],
+                                rhs=xg_w[:, js].bitcast(E2M1), rhs_scale=xg_s[:, js], start=True, stop=True)
+            if bank == 1:
+                nc.scalar.activation(out=a_sb[t][:, js], in_=a_ps[:], func=COPY)
+            else:
+                nc.vector.tensor_copy(a_sb[t][:, js], a_ps[:])
+        for t in range(PACK):
+            nc.scalar.activation(out=hid[:, t : PACK * O : PACK], in_=a_sb[t][:].indirect(o_list[:]), func=COPY,
                                  scale=sa_t[:, t : t + 1])
 
         hid_w = tile("hid_w", O, U32)
         hid_s = tile("hid_s", O, U8)
         nc.vector.quantize_mx(out=hid_w[:].bitcast(E5M2), scales=hid_s[:], in_=hid[:])
 
-        for h in range(2):
-            cols = slice(P * h, P * (h + 1))
-            sides = (
-                (wb_w[:, cols].bitcast(E4M3), wb_s[:, cols], so_t, pa_list),
-                (wc_w[:, 2 * P * h : 2 * P * (h + 1)].bitcast(E2M1), wc_s[:, cols], sp_t, pb_list),
-            )
-            for s, (words, scales, weight, places) in enumerate(sides):
-                y_ps = ps.tile([P, O], F32, name="y_ps_%d_%d" % (s, h), tag="bank_%d" % (4 + 2 * h + s))
+        for s, (weight, columns) in enumerate(((so_t, pa_list), (sp_t, pb_list))):
+            for h in range(2):
+                cols = slice(P * h, P * (h + 1))
+                if s == 0:
+                    words, scales = wb_w[:, cols].bitcast(E4M3), wb_s[:, cols]
+                else:
+                    words, scales = wc_w[:, 2 * P * h : 2 * P * (h + 1)].bitcast(E2M1), wc_s[:, cols]
+                y_ps = ps.tile([P, O], F32, name="y_ps_%d_%d" % (s, h), tag="bank_%d" % ((6 + 2 * s + h) % 8))
                 nc.tensor.matmul_mx(out=y_ps[:], lhsT=words, lhsT_scale=scales, rhs=hid_w[:].bitcast(E5M2),
                                     rhs_scale=hid_s[:], start=True, stop=True)
                 y_sb = tile("y_sb_%d_%d" % (s, h), O, F32)
                 nc.vector.tensor_copy(y_sb[:], y_ps[:])
-                nc.scalar.activation(out=pages[s][h][:].indirect(places[:]), in_=y_sb[:], func=COPY,
+                nc.scalar.activation(out=pages[s][h][:].indirect(columns[:]), in_=y_sb[:], func=COPY,
                                      scale=weight[:, h : h + 1])
-            queues = (nc.sync,) if h == 0 else (nc.sync, nc.scalar)
+
+        for h, queues in enumerate(((nc.sync,), (nc.sync, nc.scalar))):
             for c, queue in enumerate(queues):
-                half = slice(E // len(queues) * c, E // len(queues) * (c + 1))
+                part = slice(E // len(queues) * c, E // len(queues) * (c + 1))
                 best = tile("best_%d_%d" % (h, c), E // len(queues), F32)
-                nc.vector.tensor_tensor(best[:], pages[0][h][:, half], pages[1][h][:, half], MAX)
-                queue.dma_start(out=out[cols, half], in_=best[:])
+                nc.vector.tensor_tensor(best[:], pages[0][h][:, part], pages[1][h][:, part], MAX)
+                queue.dma_start(out=out[P * h : P * (h + 1), part], in_=best[:])

@@ -9,6 +9,7 @@ P = 128
 PACK = 4
 QUADS = 4
 QUAD = 32
+RUN = O // 2
 
 F32 = mybir.dt.float32
 BF16 = mybir.dt.bfloat16
@@ -60,6 +61,10 @@ def tile_list_twooutcomes_kernel(tc, xt_words, xt_scales, wt_words, wt_scales, s
         nc.vector.memset(xt_s[:].bitcast(I32), 0)
         nc.vector.memset(wb_s[:].bitcast(I32), 0)
         nc.vector.memset(wc_s[:].bitcast(I32), 0)
+        hid_w = tile("hid_w", RUN + O, U32)
+        hid_s = tile("hid_s", RUN + O, U8)
+        nc.vector.memset(hid_w[:, 0:RUN].bitcast(I32), 0)
+        nc.vector.memset(hid_s[:, 0:RUN].bitcast(I32), 0)
         for h in range(2):
             for s in range(2):
                 nc.vector.memset(pages[s][h][:], 0.0)
@@ -107,28 +112,31 @@ def tile_list_twooutcomes_kernel(tc, xt_words, xt_scales, wt_words, wt_scales, s
                 nc.scalar.activation(out=a_sb[t][:, js], in_=a_ps[:], func=COPY)
             else:
                 nc.vector.tensor_copy(a_sb[t][:, js], a_ps[:])
-        for t in range(PACK):
-            nc.scalar.activation(out=hid[:, t : PACK * O : PACK], in_=a_sb[t][:].indirect(o_list[:]), func=COPY,
-                                 scale=sa_t[:, t : t + 1])
+        for run, t in ((0, 0), (1, 0), (0, 1), (0, 2), (1, 1), (0, 3), (1, 2), (1, 3)):
+            nc.scalar.activation(out=hid[:, PACK * RUN * run + t : PACK * RUN * (run + 1) : PACK],
+                                 in_=a_sb[t][:].indirect(o_list[:, RUN // 16 * run : RUN // 16 * (run + 1)]),
+                                 func=COPY, scale=sa_t[:, t : t + 1])
+        for run in range(2):
+            cols = slice(RUN * (run + 1), RUN * (run + 2))
+            nc.vector.quantize_mx(out=hid_w[:, cols].bitcast(E5M2), scales=hid_s[:, cols],
+                                  in_=hid[:, PACK * RUN * run : PACK * RUN * (run + 1)])
 
-        hid_w = tile("hid_w", O, U32)
-        hid_s = tile("hid_s", O, U8)
-        nc.vector.quantize_mx(out=hid_w[:].bitcast(E5M2), scales=hid_s[:], in_=hid[:])
-
-        for s, (weight, columns) in enumerate(((so_t, pa_list), (sp_t, pb_list))):
-            for h in range(2):
-                cols = slice(P * h, P * (h + 1))
-                if s == 0:
-                    words, scales = wb_w[:, cols].bitcast(E4M3), wb_s[:, cols]
-                else:
-                    words, scales = wc_w[:, 2 * P * h : 2 * P * (h + 1)].bitcast(E2M1), wc_s[:, cols]
-                y_ps = ps.tile([P, O], F32, name="y_ps_%d_%d" % (s, h), tag="bank_%d" % ((6 + 2 * s + h) % 8))
-                nc.tensor.matmul_mx(out=y_ps[:], lhsT=words, lhsT_scale=scales, rhs=hid_w[:].bitcast(E5M2),
-                                    rhs_scale=hid_s[:], start=True, stop=True)
-                y_sb = tile("y_sb_%d_%d" % (s, h), O, F32)
-                nc.vector.tensor_copy(y_sb[:], y_ps[:])
-                nc.scalar.activation(out=pages[s][h][:].indirect(columns[:]), in_=y_sb[:], func=COPY,
-                                     scale=weight[:, h : h + 1])
+        outcomes = ((0, 0, 0, 0, RUN), (0, 1, RUN, 0, O), (0, 0, RUN, RUN, RUN), (1, 0, RUN, 0, O), (1, 1, RUN, 0, O))
+        for i, (s, h, first, place, count) in enumerate(outcomes):
+            cols = slice(P * h, P * (h + 1))
+            if s == 0:
+                words, scales, weight, columns = wb_w[:, cols].bitcast(E4M3), wb_s[:, cols], so_t, pa_list
+            else:
+                words, scales = wc_w[:, 2 * P * h : 2 * P * (h + 1)].bitcast(E2M1), wc_s[:, cols]
+                weight, columns = sp_t, pb_list
+            y_ps = ps.tile([P, O], F32, name="y_ps_%d" % i, tag="bank_%d" % ((6 + i) % 8))
+            nc.tensor.matmul_mx(out=y_ps[:], lhsT=words, lhsT_scale=scales,
+                                rhs=hid_w[:, first : first + O].bitcast(E5M2), rhs_scale=hid_s[:, first : first + O],
+                                start=True, stop=True)
+            y_sb = tile("y_sb_%d" % i, count, F32)
+            nc.vector.tensor_copy(y_sb[:], y_ps[:, O - count : O])
+            nc.scalar.activation(out=pages[s][h][:].indirect(columns[:, place // 16 : (place + count) // 16]),
+                                 in_=y_sb[:], func=COPY, scale=weight[:, h : h + 1])
 
         for h, queues in enumerate(((nc.sync,), (nc.sync, nc.scalar))):
             for c, queue in enumerate(queues):

from contextlib import ExitStack

import concourse.mybir as mybir

K, T, J, R, V, O, N, E = 512, 1024, 256, 512, 1024, 128, 256, 256
FLOPS = 2 * K * R * J + 2 * 2 * R * N * O

P = 128
PACK = 4
QUADS = 4
QUAD = 32
RUN = O // 2

F32 = mybir.dt.float32
BF16 = mybir.dt.bfloat16
I32 = mybir.dt.int32
U32 = mybir.dt.uint32
U16 = mybir.dt.uint16
U8 = mybir.dt.uint8
E4M3 = mybir.dt.float8_e4m3fn_x4
E5M2 = mybir.dt.float8_e5m2_x4
E2M1 = mybir.dt.float4_e2m1fn_x4
COPY = mybir.ActivationFunctionType.Copy
MAX = mybir.AluOpType.max


def tile_list_twooutcomes_kernel(tc, xt_words, xt_scales, wt_words, wt_scales, sa, wb_words, wb_scales,
                                     wc_words, wc_scales, so, sp, offs, offs2, offs3, offs4, offs5, out):
    nc = tc.nc
    with ExitStack() as ctx:
        sb = ctx.enter_context(tc.tile_pool(name="sb", bufs=1))
        ps = ctx.enter_context(tc.psum_pool(name="ps", bufs=1))

        def tile(name, cols, dtype):
            return sb.tile([P, cols], dtype, name=name, align_bytes=64)

        def load_scale_rows(queues, plane, scales):
            for q, queue in enumerate(queues):
                queue.dma_start(out=plane[QUAD * q : QUAD * q + 4, :].bitcast(I32),
                                in_=scales[0, 4 * q : 4 * q + 4, :].bitcast(I32))

        r_list = tile("r_list", R // 16, U16)
        j_list = tile("j_list", J // 16, U16)
        o_list = tile("o_list", O // 16, U16)
        pa_list = tile("pa_list", O // 16, U16)
        pb_list = tile("pb_list", O // 16, U16)
        wt_w = tile("wt_w", V, U32)
        wt_s = tile("wt_s", V, U8)
        xt_w = tile("xt_w", T, U16)
        xt_s = tile("xt_s", T, U8)
        wb_w = tile("wb_w", N, U32)
        wb_s = tile("wb_s", N, U8)
        wc_w = tile("wc_w", 2 * N, U8)
        wc_s = tile("wc_s", N, U8)
        sa_t = tile("sa_t", PACK, F32)
        so_t = tile("so_t", 2, F32)
        sp_t = tile("sp_t", 2, F32)
        pages = [[tile("page_%d_%d" % (s, h), E, F32) for h in range(2)] for s in range(2)]

        nc.vector.memset(wt_s[:].bitcast(I32), 0)
        nc.vector.memset(xt_s[:].bitcast(I32), 0)
        nc.vector.memset(wb_s[:].bitcast(I32), 0)
        nc.vector.memset(wc_s[:].bitcast(I32), 0)
        hid_w = tile("hid_w", RUN + O, U32)
        hid_s = tile("hid_s", RUN + O, U8)
        nc.vector.memset(hid_w[:, 0:RUN].bitcast(I32), 0)
        nc.vector.memset(hid_s[:, 0:RUN].bitcast(I32), 0)
        for h in range(2):
            for s in range(2):
                nc.vector.memset(pages[s][h][:], 0.0)

        nc.sync.dma_start(out=xt_w[:].bitcast(I32), in_=xt_words[0].bitcast(I32))
        nc.sync.dma_start(j_list[:], offs2)
        nc.sync.dma_start(r_list[:], offs)
        load_scale_rows([nc.scalar, nc.sync, nc.scalar, nc.sync], wt_s, wt_scales)
        nc.sync.dma_start(out=wt_w[:].bitcast(I32), in_=wt_words[0].rearrange("p n t -> p (n t)").bitcast(I32))
        load_scale_rows([nc.sync] * QUADS, xt_s, xt_scales)
        nc.sync.dma_start(o_list[:], offs3)
        nc.sync.dma_start(out=sa_t[:], in_=sa.rearrange("(p t) o -> p (t o)", t=PACK))
        nc.sync.dma_start(out=wb_w[:].bitcast(I32), in_=wb_words[0].rearrange("p n t -> p (n t)").bitcast(I32))
        nc.sync.dma_start(out=wc_w[:].bitcast(I32), in_=wc_words[0].bitcast(I32))
        load_scale_rows([nc.sync] * QUADS, wb_s, wb_scales)
        nc.sync.dma_start(pa_list[:], offs4)
        with nc.allow_non_contiguous_dma(reason="one value a partition and half"):
            nc.sync.dma_start(out=so_t[:], in_=so.rearrange("(h p) o -> p (h o)", h=2))
        load_scale_rows([nc.sync] * QUADS, wc_s, wc_scales)
        nc.sync.dma_start(pb_list[:], offs5)
        with nc.allow_non_contiguous_dma(reason="one value a partition and half"):
            nc.sync.dma_start(out=sp_t[:], in_=sp.rearrange("(h p) o -> p (h o)", h=2))

        wg_w = tile("wg_w", R, U32)
        wg_s = tile("wg_s", R, U8)
        xg_w = tile("xg_w", J, U16)
        xg_s = tile("xg_s", J, U8)
        nc.vector.tensor_copy(xg_w[:], xt_w[:].indirect(j_list[:]))
        nc.vector.tensor_copy(wg_s[:].rearrange("p (t q) -> p q t", t=PACK), wt_s[:].indirect(r_list[:]))
        nc.vector.tensor_copy(wg_w[:].rearrange("p (t q) -> p q t", t=PACK), wt_w[:].indirect(r_list[:]))
        for c in range(2):
            nc.vector.tensor_copy(xg_s[:, J // 2 * c : J // 2 * (c + 1)],
                                  xt_s[:].indirect(j_list[:, J // 32 * c : J // 32 * (c + 1)]))

        hid = tile("hid", PACK * O, BF16)
        a_sb = [tile("a_sb_%d" % t, J, F32) for t in range(PACK)]
        halves = (slice(0, J // 2), slice(J // 2, J))
        products = [(t, js) for js in halves for t in range(2)] + [(t, slice(0, J)) for t in range(2, PACK)]
        for bank, (t, js) in enumerate(products):
            cols = slice(P * t, P * (t + 1))
            a_ps = ps.tile([P, js.stop - js.start], F32, name="a_ps_%d" % bank, tag="bank_%d" % bank)
            nc.tensor.matmul_mx(out=a_ps[:], lhsT=wg_w[:, cols].bitcast(E5M2), lhsT_scale=wg_s[:, cols],
                                rhs=xg_w[:, js].bitcast(E2M1), rhs_scale=xg_s[:, js], start=True, stop=True)
            if bank == 1:
                nc.scalar.activation(out=a_sb[t][:, js], in_=a_ps[:], func=COPY)
            else:
                nc.vector.tensor_copy(a_sb[t][:, js], a_ps[:])
        for run, t in ((0, 0), (1, 0), (0, 1), (0, 2), (1, 1), (0, 3), (1, 2), (1, 3)):
            nc.scalar.activation(out=hid[:, PACK * RUN * run + t : PACK * RUN * (run + 1) : PACK],
                                 in_=a_sb[t][:].indirect(o_list[:, RUN // 16 * run : RUN // 16 * (run + 1)]),
                                 func=COPY, scale=sa_t[:, t : t + 1])
        for run in range(2):
            cols = slice(RUN * (run + 1), RUN * (run + 2))
            nc.vector.quantize_mx(out=hid_w[:, cols].bitcast(E5M2), scales=hid_s[:, cols],
                                  in_=hid[:, PACK * RUN * run : PACK * RUN * (run + 1)])

        outcomes = ((0, 0, 0, 0, RUN), (0, 1, RUN, 0, O), (0, 0, RUN, RUN, RUN), (1, 0, RUN, 0, O), (1, 1, RUN, 0, O))
        for i, (s, h, first, place, count) in enumerate(outcomes):
            cols = slice(P * h, P * (h + 1))
            if s == 0:
                words, scales, weight, columns = wb_w[:, cols].bitcast(E4M3), wb_s[:, cols], so_t, pa_list
            else:
                words, scales = wc_w[:, 2 * P * h : 2 * P * (h + 1)].bitcast(E2M1), wc_s[:, cols]
                weight, columns = sp_t, pb_list
            y_ps = ps.tile([P, O], F32, name="y_ps_%d" % i, tag="bank_%d" % ((6 + i) % 8))
            nc.tensor.matmul_mx(out=y_ps[:], lhsT=words, lhsT_scale=scales,
                                rhs=hid_w[:, first : first + O].bitcast(E5M2), rhs_scale=hid_s[:, first : first + O],
                                start=True, stop=True)
            y_sb = tile("y_sb_%d" % i, count, F32)
            nc.vector.tensor_copy(y_sb[:], y_ps[:, O - count : O])
            nc.scalar.activation(out=pages[s][h][:].indirect(columns[:, place // 16 : (place + count) // 16]),
                                 in_=y_sb[:], func=COPY, scale=weight[:, h : h + 1])

        for h, queues in enumerate(((nc.sync,), (nc.sync, nc.scalar))):
            for c, queue in enumerate(queues):
                part = slice(E // len(queues) * c, E // len(queues) * (c + 1))
                best = tile("best_%d_%d" % (h, c), E // len(queues), F32)
                nc.vector.tensor_tensor(best[:], pages[0][h][:, part], pages[1][h][:, part], MAX)
                queue.dma_start(out=out[P * h : P * (h + 1), part], in_=best[:])
